import numpy as np
import ml_dtypes


def mxq(x, axis, fmt="e4m3"):
    dtype, down = {"e4m3": (ml_dtypes.float8_e4m3fn, 7), "e5m2": (ml_dtypes.float8_e5m2, 14)}[fmt]
    v = np.moveaxis(np.asarray(x, np.float32).astype(ml_dtypes.bfloat16).astype(np.float64), axis, -1)
    blocks = v.reshape(v.shape[:-1] + (-1, 32))
    amax = np.abs(blocks).max(-1, keepdims=True)
    byte = np.maximum(np.where(amax > 0, np.frexp(amax)[1] - 1 + 127, 0) - down, 1)
    scale = np.exp2(byte - 127.0)
    codes = (blocks / scale).astype(np.float32).astype(dtype).astype(np.float64)
    return np.moveaxis((codes * scale).reshape(v.shape), -1, axis)


WIDE = False


def mx_kscale(k):
    if not WIDE:
        return np.ones(k)
    levels = np.array([10, -10, 5, -5, 0])
    if k % 512:
        return np.exp2(np.random.permutation(np.resize(levels, k // 32))).repeat(32)
    a = np.empty((k // 512, 16))
    for p in range(k // 512):
        a[p, :8] = np.random.permutation(np.resize(levels, 8))
        for g in range(8):
            far = levels[np.abs(levels - a[p, g]) >= 10]
            a[p, g + 8] = far[np.random.randint(len(far))]
    return np.exp2(a.ravel()).repeat(32)


def f64(x):
    return np.asarray(x).astype(np.float64)


def striped(idx):
    return np.tile(np.asarray(idx).reshape(-1, 16).T, (8, 1)).astype(np.uint16)


def unstriped(offs):
    return offs[:16].T.reshape(-1).astype(np.int64)


E2M1 = np.array([0.0, 0.5, 1.0, 1.5, 2.0, 3.0, 4.0, 6.0, -0.0, -0.5, -1.0, -1.5, -2.0, -3.0, -4.0, -6.0])


def pack_weight(w, fmt):
    k, n = w.shape
    w = f64(np.asarray(w, np.float32).astype(ml_dtypes.bfloat16)).reshape(k // 32, 32, n)
    amax = np.abs(w).max(1)
    if fmt == "e4m3":
        byte = np.frexp(amax)[1] - 1 + 127 - 7
    else:
        mant, ex = np.frexp(amax / 6.0)
        byte = np.where(mant > 0.5, ex, ex - 1) + 127
    byte = np.clip(np.where(amax > 0, byte, 1), 1, 254)
    scaled = (w * np.exp2(127.0 - byte)[:, None, :]).reshape(k, n).astype(np.float32)
    by_word = np.ascontiguousarray(scaled.reshape(k // 512, 128, 4, n).transpose(0, 1, 3, 2))
    if fmt == "e4m3":
        words = by_word.astype(ml_dtypes.float8_e4m3fn).view(np.uint8)
    else:
        c = by_word.astype(ml_dtypes.float4_e2m1fn).view(np.uint8) & 0xF
        words = (c[..., 0::2] | (c[..., 1::2] << 4)).reshape(k // 512, 128, 2 * n)
    return np.ascontiguousarray(words), np.ascontiguousarray(byte.astype(np.uint8).reshape(k // 512, 16, n))


def unpack_weight(words, scales, fmt):
    g, _, n = scales.shape
    words = np.ascontiguousarray(words).reshape(g, 128, n, -1)
    if fmt == "e4m3":
        vals = words.view(ml_dtypes.float8_e4m3fn).astype(np.float64)
    else:
        nib = np.empty((g, 128, n, 4), np.uint8)
        nib[..., 0::2] = words & 0xF
        nib[..., 1::2] = words >> 4
        vals = E2M1[nib]
    vals = vals * np.repeat(np.exp2(scales.astype(np.float64) - 127.0), 8, axis=1)[..., None]
    return vals.transpose(0, 1, 3, 2).reshape(g * 512, n)


def sigmoid(v):
    return 1.0 / (1.0 + np.exp(-v))


def bf(x):
    return np.asarray(x, np.float32).astype(ml_dtypes.bfloat16)


def planes(Y):
    r, m = Y.shape
    b = f64(bf(Y)).reshape(r // 32, 32, m)
    amax = np.abs(b).max(1)
    byte = np.clip(np.where(amax > 0, np.frexp(amax)[1] - 1 + 127 - 7, 1), 1, 254)
    codes = (b * np.exp2(127.0 - byte)[:, None, :]).reshape(r, m).astype(np.float32).astype(ml_dtypes.float8_e4m3fn).view(np.uint8)
    words = codes.reshape(r // 512, 128, 4, m).transpose(0, 1, 3, 2)
    return np.ascontiguousarray(words), np.ascontiguousarray(byte.astype(np.uint8).reshape(r // 512, 16, m))


K, T, R, J, M = 512, 512, 2048, 512, 512


def setup_inputs():
    n = np.random.standard_normal
    idx = np.random.permutation(R)[:J]
    fk = mx_kscale(K)
    fj = mx_kscale(J)
    tj = np.ones(R)
    tj[idx] = fj
    wup = pack_weight(n((K, R)) * 1 / np.sqrt(K) * fk[:, None], "e2m1")
    wgp = pack_weight(n((K, R)) * 1 / np.sqrt(K) * fk[:, None] * tj, "e4m3")
    return {
        "xt": (n((K, T)) / fk[:, None]).astype(np.float32),
        "wu_words": wup[0],
        "wu_scales": wup[1],
        "wg_words": wgp[0],
        "wg_scales": wgp[1],
        "wd": (n((M, R)) * (1 / np.sqrt(J)) / tj).astype(np.float32),
        "rw": (np.random.uniform(0.5, 2.0, (1, T))).astype(np.float32),
        "offs": striped(idx),
    }


def reference(xt, wu_words, wu_scales, wg_words, wg_scales, wd, rw, offs):
    idx = unstriped(offs)
    wuu = unpack_weight(wu_words, wu_scales, "e2m1")
    wgu = unpack_weight(wg_words, wg_scales, "e4m3")
    wuidxg = wuu[:, idx]
    xtq = mxq(f64(xt), 0, "e4m3")
    a = wuidxg.T @ xtq
    wgidxg = wgu[:, idx]
    b = wgidxg.T @ xtq
    hid = sigmoid(a) * b
    dj = f64(wd)[:, idx].T
    djq = mxq(dj, 0, "e4m3")
    hidq = mxq(hid, 0, "e4m3")
    p = djq.T @ hidq
    y = p * f64(rw)
    words, scales = planes(y)
    return y, words, scales

@@ -1,0 +1,265 @@
+from contextlib import ExitStack
+
+import concourse.mybir as mybir
+from concourse.masks import make_identity
+
+K, T, R, J, M = 512, 512, 2048, 512, 512
+FLOPS = 2 * (2 * K * J * T + J * M * T)
+
+F32 = mybir.dt.float32
+BF16 = mybir.dt.bfloat16
+I32 = mybir.dt.int32
+U32 = mybir.dt.uint32
+U16 = mybir.dt.uint16
+U8 = mybir.dt.uint8
+FP8X4 = mybir.dt.float8_e4m3fn_x4
+FP4X4 = mybir.dt.float4_e2m1fn_x4
+ACT = mybir.ActivationFunctionType
+MULT = mybir.AluOpType.mult
+
+P = 128
+PACK = 4
+CHUNK = 128
+N_CHUNKS = T // CHUNK
+BLOCKS = J // 32
+RUN = 8
+
+
+def tile_list_hot_neurons_product_pl_kernel(
+    tc, xt, wu_words, wu_scales, wg_words, wg_scales, wd, rw, offs, out_0, out_1, out_2
+):
+    nc = tc.nc
+    with ExitStack() as ctx:
+        keep = ctx.enter_context(tc.tile_pool(name="keep", bufs=1))
+        late = ctx.enter_context(tc.tile_pool(name="late", bufs=1))
+        ring = ctx.enter_context(tc.tile_pool(name="ring", bufs=2))
+        ps_a = ctx.enter_context(tc.psum_pool(name="ps_a", bufs=2))
+        ps_b = ctx.enter_context(tc.psum_pool(name="ps_b", bufs=2))
+        ps_t = ctx.enter_context(tc.psum_pool(name="ps_t", bufs=1))
+        ps_p = ctx.enter_context(tc.psum_pool(name="ps_p", bufs=3))
+
+        offsets = keep.tile([P, J // 16], U16, name="offsets")
+        nc.sync.dma_start(offsets[:], offs)
+
+        su_win = keep.tile([P, R], U8, name="su_win")
+        sg_win = keep.tile([P, R], U8, name="sg_win")
+        nc.vector.memset(su_win[:].bitcast(I32), 0)
+        nc.vector.memset(sg_win[:].bitcast(I32), 0)
+        w_scales = keep.tile([P, 2 * J], U8, name="w_scales", align_bytes=64)
+        nc.gpsimd.memset(w_scales[:].bitcast(I32), 0)
+        nc.scalar.dma_start(su_win[0:P:8, :].bitcast(I32), wu_scales[0].bitcast(I32))
+        nc.scalar.dma_start(sg_win[0:P:8, :].bitcast(I32), wg_scales[0].bitcast(I32))
+        rw_col = keep.tile([P, PACK], F32, name="rw_col")
+        nc.scalar.dma_start(rw_col[:], rw[0].rearrange("(p c) -> p c", c=PACK))
+
+        wu_win = keep.tile([P, R], U16, name="wu_win")
+        nc.sync.dma_start(wu_win[:].bitcast(I32), wu_words[0].bitcast(I32))
+        x_rows = xt.rearrange("(p i) t -> p i t", i=PACK)
+        x_raw = [keep.tile([P, PACK, T // 2], F32, name="x_raw%d" % h) for h in range(2)]
+        nc.sync.dma_start(x_raw[0][:], x_rows[:, :, 0 : T // 2])
+        wg_win = keep.tile([P, R], I32, name="wg_win", tag="wg_win")
+        nc.sync.dma_start(wg_win[:], wg_words[0].rearrange("p n t -> p (n t)").bitcast(I32))
+        nc.sync.dma_start(x_raw[1][:], x_rows[:, :, T // 2 : T])
+        wd_rows = wd.rearrange("(p i) r -> p i r", i=PACK)
+        wd_win = []
+
+        def load_wd(i, tag):
+            if i == PACK - 1:
+                win = late.tile([P, R], F32, name="wd_last", offset=0)
+            elif tag == "late":
+                win = late.tile([P, R], F32, name="wd_first", offset=0)
+            else:
+                win = keep.tile([P, R], F32, name="wd_win%d" % i, tag=tag)
+            nc.sync.dma_start(win[:], wd_rows[:, i, :])
+            wd_win.append(win)
+
+
+        ident_f = keep.tile([P, P], F32, name="ident_f")
+        make_identity(nc, ident_f[:])
+        ident_b = keep.tile([P, P], BF16, name="ident_b")
+        make_identity(nc, ident_b[:])
+        warm = keep.tile([P, 1], F32, name="warm")
+        nc.scalar.activation(warm[:], ident_b[:, 0:1], ACT.Sigmoid)
+
+        rw_ps = ps_t.tile([P, PACK, P], F32, name="turned")
+        for c in range(PACK):
+            nc.tensor.transpose(rw_ps[:, c, :], rw_col[:, c : c + 1].to_broadcast([P, P]), ident_f[:])
+        rw_all = keep.tile([P, P, PACK], F32, name="rw_all")
+        nc.scalar.copy(rw_all[:], rw_ps[:].rearrange("p c n -> p n c"))
+        rw_row = rw_all[:].rearrange("p n c -> p (n c)")
+
+        su_got = keep.tile([P, J], U8, name="su_got")
+        nc.vector.tensor_copy(su_got[:], su_win[:].indirect(offsets[:]))
+        sg_got = keep.tile([P, J], U8, name="sg_got", tag="sg_got")
+        nc.vector.tensor_copy(sg_got[:], sg_win[:].indirect(offsets[:]))
+
+        def deal(dst, src):
+            nc.vector.tensor_copy(
+                dst.bitcast(I32).rearrange("p (t b w) -> p t b w", t=PACK, b=BLOCKS),
+                src.bitcast(I32).rearrange("p (b t w) -> p t b w", t=PACK, b=BLOCKS),
+            )
+
+        s_dealt = keep.tile([P, 2 * J], U8, name="s_dealt")
+        deal(s_dealt[:, 0:J], su_got[:])
+        deal(s_dealt[:, J : 2 * J], sg_got[:])
+        for q in range(4):
+            nc.sync.dma_start(
+                w_scales[32 * q : 32 * q + 4, :].bitcast(I32), s_dealt[32 * q : 32 * q + 32 : 8, :].bitcast(I32)
+            )
+        for i in range(PACK):
+            load_wd(i, "wd%d" % i)
+
+        wu_got = keep.tile([P, J], U16, name="wu_got", tag="wu_got")
+        nc.vector.tensor_copy(wu_got[:], wu_win[:].indirect(offsets[:]))
+        wu_codes = keep.tile([P, J], U16, name="wu_codes", align_bytes=64)
+        deal(wu_codes[:], wu_got[:])
+        x_codes, x_scales = [], []
+
+        def quantise_x(h):
+            xb = keep.tile([P, T // 2, PACK], BF16, name="x_bf%d" % h, align_bytes=64)
+            nc.scalar.copy(
+                xb[:].rearrange("p (g n) i -> p g i n", n=4),
+                x_raw[h][:].rearrange("p i (g n) -> p g i n", n=4),
+            )
+            xc = keep.tile([P, T // 2], U32, name="x_codes%d" % h, align_bytes=64)
+            xs = keep.tile([P, T // 2], U8, name="x_scales%d" % h, align_bytes=64)
+            nc.vector.quantize_mx(xc[:].bitcast(FP8X4), xs[:], xb[:].rearrange("p n i -> p (n i)"))
+            for c in range(2):
+                x_codes.append(xc[:, c * CHUNK : (c + 1) * CHUNK])
+                x_scales.append(xs[:, c * CHUNK : (c + 1) * CHUNK])
+
+        quantise_x(0)
+        wg_codes = keep.tile([P, J], U32, name="wg_codes", align_bytes=64)
+        nc.vector.tensor_copy(
+            wg_codes[:].rearrange("p (t b r) -> p b t r", t=PACK, r=RUN),
+            wg_win[:].bitcast(U32).indirect(offsets[:]),
+        )
+
+        quantise_x(1)
+
+        h_codes = keep.tile([P, T], U32, name="h_codes", align_bytes=64)
+        h_scales = keep.tile([P, T], U8, name="h_scales", align_bytes=64)
+
+        def first_stage(c):
+            a_ps = ps_a.tile([P, PACK, CHUNK], F32, name="a_ps")
+            b_ps = ps_b.tile([P, PACK, CHUNK], F32, name="b_ps")
+            for t in range(PACK):
+                nc.tensor.matmul_mx(
+                    a_ps[:, t, :],
+                    lhsT=wu_codes[:, t * P : (t + 1) * P].bitcast(FP4X4),
+                    lhsT_scale=w_scales[:, t * P : (t + 1) * P],
+                    rhs=x_codes[c].bitcast(FP8X4),
+                    rhs_scale=x_scales[c],
+                    start=True,
+                    stop=True,
+                )
+            for t in range(PACK):
+                nc.tensor.matmul_mx(
+                    b_ps[:, t, :],
+                    lhsT=wg_codes[:, t * P : (t + 1) * P].bitcast(FP8X4),
+                    lhsT_scale=w_scales[:, J + t * P : J + (t + 1) * P],
+                    rhs=x_codes[c].bitcast(FP8X4),
+                    rhs_scale=x_scales[c],
+                    start=True,
+                    stop=True,
+                )
+            gate = ring.tile([P, CHUNK, PACK], F32, name="gate")
+            nc.scalar.activation(gate[:], a_ps[:].rearrange("p t n -> p n t"), ACT.Sigmoid)
+            hid = ring.tile([P, CHUNK, PACK], BF16, name="hid", align_bytes=64)
+            nc.vector.tensor_tensor(hid[:], b_ps[:].rearrange("p t n -> p n t"), gate[:], MULT)
+            return hid
+
+        def quantise_hid(c, hid):
+            cols = slice(c * CHUNK, (c + 1) * CHUNK)
+            nc.vector.quantize_mx(
+                h_codes[:, cols].bitcast(FP8X4), h_scales[:, cols], hid[:].rearrange("p n t -> p (n t)")
+            )
+
+        def gather_wd(i, d_bf):
+            got = ring.tile([P, PACK, P], BF16, name="d_got")
+            nc.vector.tensor_copy(
+                got[:].rearrange("p t (b r) -> p b t r", r=RUN), wd_win[i][:].indirect(offsets[:])
+            )
+            turned = ps_t.tile([P, PACK, P], BF16, name="turned")
+            for t in range(PACK):
+                nc.tensor.transpose(turned[:, t, :], got[:, t, :], ident_b[:])
+            nc.scalar.copy(d_bf, turned[:].rearrange("p t m -> p m t"))
+
+        def quantise_d(dc, ds, d_bf):
+            nc.vector.quantize_mx(dc.bitcast(FP8X4), ds, d_bf.rearrange("p m t -> p (m t)"))
+
+        out_rows = out_0.rearrange("(p i) t -> p i t", i=PACK)
+
+        def second_stage(i, dc, ds, parts):
+            width = T // parts
+            for h in range(parts):
+                cols = slice(h * width, (h + 1) * width)
+                p_ps = ps_p.tile([P, width], F32, name="p_ps")
+                nc.tensor.matmul_mx(
+                    p_ps[:],
+                    lhsT=dc.bitcast(FP8X4),
+                    lhsT_scale=ds,
+                    rhs=h_codes[:, cols].bitcast(FP8X4),
+                    rhs_scale=h_scales[:, cols],
+                    start=True,
+                    stop=True,
+                )
+                nc.vector.tensor_tensor(y[:, i, cols], p_ps[:], rw_row[:, cols], MULT)
+            nc.sync.dma_start(out_rows[:, i, :], y[:, i, :])
+
+        d_bf0 = keep.tile([P, P, PACK], BF16, name="d_bf0", align_bytes=64)
+        d_bf12 = keep.tile([P, 2 * P, PACK], BF16, name="d_bf12", align_bytes=64)
+        d_bf3 = keep.tile([P, P, PACK], BF16, name="d_bf3", align_bytes=64)
+        dc0 = keep.tile([P, P], U32, name="dc0", align_bytes=64)
+        ds0 = keep.tile([P, P], U8, name="ds0", align_bytes=64)
+        dc3 = keep.tile([P, P], U32, name="dc3", align_bytes=64)
+        ds3 = keep.tile([P, P], U8, name="ds3", align_bytes=64)
+        ds12 = keep.tile([P, 2 * P], U8, name="ds12", align_bytes=64)
+
+        hid0 = first_stage(0)
+        gather_wd(0, d_bf0[:])
+        hid1 = first_stage(1)
+        quantise_hid(0, hid0)
+        hid2 = first_stage(2)
+        quantise_hid(1, hid1)
+        quantise_d(dc0[:], ds0[:], d_bf0[:])
+        gather_wd(1, d_bf12[:, 0:P, :])
+        hid3 = first_stage(3)
+        quantise_hid(2, hid2)
+        quantise_hid(3, hid3)
+        gather_wd(2, d_bf12[:, P : 2 * P, :])
+        gather_wd(3, d_bf3[:])
+        dc12 = late.tile([P, 2 * P], U32, name="dc12", offset=0, align_bytes=64)
+        y = late.tile([P, PACK, T], F32, name="y", offset=1024)
+        quantise_d(dc12[:], ds12[:], d_bf12[:])
+        second_stage(0, dc0[:], ds0[:], 1)
+        second_stage(1, dc12[:, 0:P], ds12[:, 0:P], 1)
+        quantise_d(dc3[:], ds3[:], d_bf3[:])
+        second_stage(2, dc12[:, P : 2 * P], ds12[:, P : 2 * P], 1)
+        second_stage(3, dc3[:], ds3[:], 2)
+
+        y_codes = keep.tile([P, T], U32, name="y_codes", align_bytes=64)
+        y_scales = keep.tile([P, T], U8, name="y_scales", align_bytes=64)
+        half = T // 2
+        words_out = out_1[0].rearrange("p n t -> p (n t)").bitcast(I32)
+        y_bf = []
+        for h in range(2):
+            yb = keep.tile([P, half, PACK], BF16, name="y_bf%d" % h, align_bytes=64)
+            dst = yb[:].rearrange("p (g n) i -> p g i n", n=4)
+            src = y[:, :, h * half : (h + 1) * half].rearrange("p i (g n) -> p g i n", n=4)
+            if h == 1:
+                nc.vector.tensor_copy(dst, src)
+            else:
+                nc.scalar.copy(dst, src)
+            y_bf.append(yb)
+        for h in (1, 0):
+            cols = slice(h * half, (h + 1) * half)
+            nc.vector.quantize_mx(
+                y_codes[:, cols].bitcast(FP8X4), y_scales[:, cols], y_bf[h][:].rearrange("p n i -> p (n i)")
+            )
+            nc.sync.dma_start(words_out[:, cols], y_codes[:, cols].bitcast(I32))
+        for q in range(4):
+            eng = nc.scalar if q % 2 == 0 else nc.sync
+            eng.dma_start(
+                out_2[0, 4 * q : 4 * q + 4, :].bitcast(I32), y_scales[32 * q : 32 * q + 4, :].bitcast(I32)
+            )

@@ -34,23 +34,22 @@ def tile_list_hot_neurons_product_pl_kernel(
         late = ctx.enter_context(tc.tile_pool(name="late", bufs=1))
         ring = ctx.enter_context(tc.tile_pool(name="ring", bufs=2))
         ps_a = ctx.enter_context(tc.psum_pool(name="ps_a", bufs=2))
-        ps_b = ctx.enter_context(tc.psum_pool(name="ps_b", bufs=2))
-        ps_t = ctx.enter_context(tc.psum_pool(name="ps_t", bufs=1))
-        ps_p = ctx.enter_context(tc.psum_pool(name="ps_p", bufs=3))
+        ps_b = ctx.enter_context(tc.psum_pool(name="ps_b", bufs=4))
+        ps_t = ctx.enter_context(tc.psum_pool(name="ps_t", bufs=2))
 
         offsets = keep.tile([P, J // 16], U16, name="offsets")
         nc.sync.dma_start(offsets[:], offs)
 
         su_win = keep.tile([P, R], U8, name="su_win")
         sg_win = keep.tile([P, R], U8, name="sg_win")
-        nc.vector.memset(su_win[:].bitcast(I32), 0)
+        nc.gpsimd.memset(su_win[:].bitcast(I32), 0)
         nc.vector.memset(sg_win[:].bitcast(I32), 0)
         w_scales = keep.tile([P, 2 * J], U8, name="w_scales", align_bytes=64)
-        nc.gpsimd.memset(w_scales[:].bitcast(I32), 0)
-        nc.scalar.dma_start(su_win[0:P:8, :].bitcast(I32), wu_scales[0].bitcast(I32))
-        nc.scalar.dma_start(sg_win[0:P:8, :].bitcast(I32), wg_scales[0].bitcast(I32))
+        nc.vector.memset(w_scales[:].bitcast(I32), 0)
         rw_col = keep.tile([P, PACK], F32, name="rw_col")
-        nc.scalar.dma_start(rw_col[:], rw[0].rearrange("(p c) -> p c", c=PACK))
+        nc.sync.dma_start(rw_col[:], rw[0].rearrange("(p c) -> p c", c=PACK))
+        nc.sync.dma_start(su_win[0:P:8, :].bitcast(I32), wu_scales[0].bitcast(I32))
+        nc.sync.dma_start(sg_win[0:P:8, :].bitcast(I32), wg_scales[0].bitcast(I32))
 
         wu_win = keep.tile([P, R], U16, name="wu_win")
         nc.sync.dma_start(wu_win[:].bitcast(I32), wu_words[0].bitcast(I32))
@@ -69,7 +68,7 @@ def tile_list_hot_neurons_product_pl_kernel(
             elif tag == "late":
                 win = late.tile([P, R], F32, name="wd_first", offset=0)
             else:
-                win = keep.tile([P, R], F32, name="wd_win%d" % i, tag=tag)
+                win = keep.tile([P, R], F32, name="wd_win%d" % i, tag=tag, align_bytes=64)
             nc.sync.dma_start(win[:], wd_rows[:, i, :])
             wd_win.append(win)
 
@@ -109,7 +108,7 @@ def tile_list_hot_neurons_product_pl_kernel(
         for i in range(PACK):
             load_wd(i, "wd%d" % i)
 
-        wu_got = keep.tile([P, J], U16, name="wu_got", tag="wu_got")
+        wu_got = keep.tile([P, J], U16, name="wu_got", tag="sg_got")
         nc.vector.tensor_copy(wu_got[:], wu_win[:].indirect(offsets[:]))
         wu_codes = keep.tile([P, J], U16, name="wu_codes", align_bytes=64)
         deal(wu_codes[:], wu_got[:])
@@ -117,7 +116,8 @@ def tile_list_hot_neurons_product_pl_kernel(
 
         def quantise_x(h):
             xb = keep.tile([P, T // 2, PACK], BF16, name="x_bf%d" % h, align_bytes=64)
-            nc.scalar.copy(
+            weave_x = nc.scalar.copy if h == 0 else nc.vector.tensor_copy
+            weave_x(
                 xb[:].rearrange("p (g n) i -> p g i n", n=4),
                 x_raw[h][:].rearrange("p i (g n) -> p g i n", n=4),
             )
@@ -140,9 +140,9 @@ def tile_list_hot_neurons_product_pl_kernel(
         h_codes = keep.tile([P, T], U32, name="h_codes", align_bytes=64)
         h_scales = keep.tile([P, T], U8, name="h_scales", align_bytes=64)
 
-        def first_stage(c):
+        def first_stage(c, gate_tag):
             a_ps = ps_a.tile([P, PACK, CHUNK], F32, name="a_ps")
-            b_ps = ps_b.tile([P, PACK, CHUNK], F32, name="b_ps")
+            b_ps = ps_b.tile([P, PACK, CHUNK], F32, name="b_ps", tag="wide")
             for t in range(PACK):
                 nc.tensor.matmul_mx(
                     a_ps[:, t, :],
@@ -163,22 +163,42 @@ def tile_list_hot_neurons_product_pl_kernel(
                     start=True,
                     stop=True,
                 )
-            gate = ring.tile([P, CHUNK, PACK], F32, name="gate")
+            gate = keep.tile([P, CHUNK, PACK], F32, name="gate%d" % c, tag=gate_tag)
             nc.scalar.activation(gate[:], a_ps[:].rearrange("p t n -> p n t"), ACT.Sigmoid)
-            hid = ring.tile([P, CHUNK, PACK], BF16, name="hid", align_bytes=64)
-            nc.vector.tensor_tensor(hid[:], b_ps[:].rearrange("p t n -> p n t"), gate[:], MULT)
-            return hid
+            return b_ps, gate
 
-        def quantise_hid(c, hid):
-            cols = slice(c * CHUNK, (c + 1) * CHUNK)
+        def hidden(hid, b_ps, gate):
+            nc.vector.tensor_tensor(hid, b_ps[:].rearrange("p t n -> p n t"), gate[:], MULT)
+
+        def quantise_hid(h, hid):
+            cols = slice(h * 2 * CHUNK, (h + 1) * 2 * CHUNK)
             nc.vector.quantize_mx(
                 h_codes[:, cols].bitcast(FP8X4), h_scales[:, cols], hid[:].rearrange("p n t -> p (n t)")
             )
 
-        def gather_wd(i, d_bf):
-            got = ring.tile([P, PACK, P], BF16, name="d_got")
+        def gather_wd(i, got_tag):
+            got = keep.tile([P, 2, P, 2], BF16, name="d_got%d" % i, tag=got_tag)
             nc.vector.tensor_copy(
-                got[:].rearrange("p t (b r) -> p b t r", r=RUN), wd_win[i][:].indirect(offsets[:])
+                got[:].rearrange("p u (b r) e -> p b u e r", r=RUN), wd_win[i][:].indirect(offsets[:])
+            )
+            return got
+
+        def turn(got, d_bf):
+            words = got[:].rearrange("p u q e -> p (u q e)").bitcast(F32)
+            turned = ps_t.tile([P, 2, P], F32, name="turned")
+            for u in range(2):
+                nc.tensor.transpose(turned[:, u, :], words[:, u * P : (u + 1) * P], ident_f[:])
+            nc.scalar.copy(
+                d_bf.rearrange("p m t -> p (m t)").bitcast(F32).rearrange("p (m u) -> p m u", u=2),
+                turned[:].rearrange("p u m -> p m u"),
+            )
+
+        def gather_and_turn_on_scalar(i, d_bf):
+            cast = keep.tile([P, R], BF16, name="wd_cast")
+            nc.scalar.activation(cast[:], wd_win[i][:], ACT.Copy)
+            got = keep.tile([P, PACK, P], BF16, name="d_got_scalar")
+            nc.scalar.activation(
+                got[:].rearrange("p t (b r) -> p b t r", r=RUN), cast[:].indirect(offsets[:]), ACT.Copy
             )
             turned = ps_t.tile([P, PACK, P], BF16, name="turned")
             for t in range(PACK):
@@ -194,7 +214,7 @@ def tile_list_hot_neurons_product_pl_kernel(
             width = T // parts
             for h in range(parts):
                 cols = slice(h * width, (h + 1) * width)
-                p_ps = ps_p.tile([P, width], F32, name="p_ps")
+                p_ps = ps_b.tile([P, width], F32, name="p_ps", tag="wide")
                 nc.tensor.matmul_mx(
                     p_ps[:],
                     lhsT=dc.bitcast(FP8X4),
@@ -216,23 +236,25 @@ def tile_list_hot_neurons_product_pl_kernel(
         ds3 = keep.tile([P, P], U8, name="ds3", align_bytes=64)
         ds12 = keep.tile([P, 2 * P], U8, name="ds12", align_bytes=64)
 
-        hid0 = first_stage(0)
-        gather_wd(0, d_bf0[:])
-        hid1 = first_stage(1)
-        quantise_hid(0, hid0)
-        hid2 = first_stage(2)
-        quantise_hid(1, hid1)
+        sums = [first_stage(c, "gate%d" % c) for c in range(N_CHUNKS)]
+        hid_a = keep.tile([P, 2 * CHUNK, PACK], BF16, name="hid_a", align_bytes=64)
+        hid_b = keep.tile([P, 2 * CHUNK, PACK], BF16, name="hid_b", align_bytes=64)
+        y = keep.tile([P, PACK, T], F32, name="y")
+        hidden(hid_a[:, 0:CHUNK, :], *sums[0])
+        got0 = gather_wd(0, "gate0")
+        hidden(hid_a[:, CHUNK : 2 * CHUNK, :], *sums[1])
+        hidden(hid_b[:, 0:CHUNK, :], *sums[2])
+        quantise_hid(0, hid_a)
+        hidden(hid_b[:, CHUNK : 2 * CHUNK, :], *sums[3])
+        turn(got0, d_bf0[:])
         quantise_d(dc0[:], ds0[:], d_bf0[:])
-        gather_wd(1, d_bf12[:, 0:P, :])
-        hid3 = first_stage(3)
-        quantise_hid(2, hid2)
-        quantise_hid(3, hid3)
-        gather_wd(2, d_bf12[:, P : 2 * P, :])
-        gather_wd(3, d_bf3[:])
-        dc12 = late.tile([P, 2 * P], U32, name="dc12", offset=0, align_bytes=64)
-        y = late.tile([P, PACK, T], F32, name="y", offset=1024)
-        quantise_d(dc12[:], ds12[:], d_bf12[:])
+        quantise_hid(1, hid_b)
+        gather_and_turn_on_scalar(1, d_bf12[:, 0:P, :])
+        turn(gather_wd(2, "got2"), d_bf12[:, P : 2 * P, :])
         second_stage(0, dc0[:], ds0[:], 1)
+        turn(gather_wd(3, "got3"), d_bf3[:])
+        dc12 = late.tile([P, 2 * P], U32, name="dc12", offset=0, align_bytes=64)
+        quantise_d(dc12[:], ds12[:], d_bf12[:])
         second_stage(1, dc12[:, 0:P], ds12[:, 0:P], 1)
         quantise_d(dc3[:], ds3[:], d_bf3[:])
         second_stage(2, dc12[:, P : 2 * P], ds12[:, P : 2 * P], 1)
@@ -242,16 +264,18 @@ def tile_list_hot_neurons_product_pl_kernel(
         y_scales = keep.tile([P, T], U8, name="y_scales", align_bytes=64)
         half = T // 2
         words_out = out_1[0].rearrange("p n t -> p (n t)").bitcast(I32)
-        y_bf = []
-        for h in range(2):
-            yb = keep.tile([P, half, PACK], BF16, name="y_bf%d" % h, align_bytes=64)
-            dst = yb[:].rearrange("p (g n) i -> p g i n", n=4)
-            src = y[:, :, h * half : (h + 1) * half].rearrange("p i (g n) -> p g i n", n=4)
-            if h == 1:
-                nc.vector.tensor_copy(dst, src)
-            else:
-                nc.scalar.copy(dst, src)
-            y_bf.append(yb)
+        y_bf = [keep.tile([P, half, PACK], BF16, name="y_bf%d" % h, align_bytes=64) for h in range(2)]
+
+        def weave(copy, h, lo, hi):
+            copy(
+                y_bf[h][:, lo:hi, :].rearrange("p (g n) i -> p g i n", n=4),
+                y[:, :, h * half + lo : h * half + hi].rearrange("p i (g n) -> p g i n", n=4),
+            )
+
+        split = 160
+        weave(nc.scalar.copy, 0, 0, split)
+        weave(nc.vector.tensor_copy, 1, 0, half)
+        weave(nc.vector.tensor_copy, 0, split, half)
         for h in (1, 0):
             cols = slice(h * half, (h + 1) * half)
             nc.vector.quantize_mx(

@@ -20,9 +20,10 @@ MULT = mybir.AluOpType.mult
 P = 128
 PACK = 4
 CHUNK = 128
-N_CHUNKS = T // CHUNK
+HALF = T // 2
 BLOCKS = J // 32
 RUN = 8
+GROUP = 4
 
 
 def tile_list_hot_neurons_product_pl_kernel(
@@ -32,7 +33,6 @@ def tile_list_hot_neurons_product_pl_kernel(
     with ExitStack() as ctx:
         keep = ctx.enter_context(tc.tile_pool(name="keep", bufs=1))
         late = ctx.enter_context(tc.tile_pool(name="late", bufs=1))
-        ring = ctx.enter_context(tc.tile_pool(name="ring", bufs=2))
         ps_a = ctx.enter_context(tc.psum_pool(name="ps_a", bufs=2))
         ps_b = ctx.enter_context(tc.psum_pool(name="ps_b", bufs=4))
         ps_t = ctx.enter_context(tc.psum_pool(name="ps_t", bufs=2))
@@ -40,38 +40,26 @@ def tile_list_hot_neurons_product_pl_kernel(
         offsets = keep.tile([P, J // 16], U16, name="offsets")
         nc.sync.dma_start(offsets[:], offs)
 
-        su_win = keep.tile([P, R], U8, name="su_win")
-        sg_win = keep.tile([P, R], U8, name="sg_win")
-        nc.gpsimd.memset(su_win[:].bitcast(I32), 0)
-        nc.vector.memset(sg_win[:].bitcast(I32), 0)
-        w_scales = keep.tile([P, 2 * J], U8, name="w_scales", align_bytes=64)
-        nc.vector.memset(w_scales[:].bitcast(I32), 0)
-        rw_col = keep.tile([P, PACK], F32, name="rw_col")
-        nc.sync.dma_start(rw_col[:], rw[0].rearrange("(p c) -> p c", c=PACK))
-        nc.sync.dma_start(su_win[0:P:8, :].bitcast(I32), wu_scales[0].bitcast(I32))
-        nc.sync.dma_start(sg_win[0:P:8, :].bitcast(I32), wg_scales[0].bitcast(I32))
+        su_win = keep.tile([P, R], U8, name="su_win", tag="su_win", align_bytes=64)
+        sg_win = keep.tile([P, R], U8, name="sg_win", tag="sg_win")
+        wg_plane = keep.tile([P, J], U8, name="wg_plane", align_bytes=64)
+        nc.gpsimd.memset(sg_win[:].bitcast(I32), 0)
+        nc.vector.memset(su_win[:].bitcast(I32), 0)
+        nc.vector.memset(wg_plane[:].bitcast(I32), 0)
 
         wu_win = keep.tile([P, R], U16, name="wu_win")
         nc.sync.dma_start(wu_win[:].bitcast(I32), wu_words[0].bitcast(I32))
+        nc.sync.dma_start(sg_win[0:P:8, :].bitcast(I32), wg_scales[0].bitcast(I32))
+        for q in (0, 2, 1, 3):
+            nc.sync.dma_start(
+                su_win[32 * q : 32 * q + 4, :].bitcast(I32), wu_scales[0, 4 * q : 4 * q + 4, :].bitcast(I32)
+            )
         x_rows = xt.rearrange("(p i) t -> p i t", i=PACK)
-        x_raw = [keep.tile([P, PACK, T // 2], F32, name="x_raw%d" % h) for h in range(2)]
-        nc.sync.dma_start(x_raw[0][:], x_rows[:, :, 0 : T // 2])
-        wg_win = keep.tile([P, R], I32, name="wg_win", tag="wg_win")
+        x_raw = [keep.tile([P, PACK, HALF], F32, name="x_raw%d" % h) for h in range(2)]
+        nc.sync.dma_start(x_raw[0][:], x_rows[:, :, 0:HALF])
+        wg_win = keep.tile([P, R], I32, name="wg_win")
         nc.sync.dma_start(wg_win[:], wg_words[0].rearrange("p n t -> p (n t)").bitcast(I32))
-        nc.sync.dma_start(x_raw[1][:], x_rows[:, :, T // 2 : T])
-        wd_rows = wd.rearrange("(p i) r -> p i r", i=PACK)
-        wd_win = []
-
-        def load_wd(i, tag):
-            if i == PACK - 1:
-                win = late.tile([P, R], F32, name="wd_last", offset=0)
-            elif tag == "late":
-                win = late.tile([P, R], F32, name="wd_first", offset=0)
-            else:
-                win = keep.tile([P, R], F32, name="wd_win%d" % i, tag=tag, align_bytes=64)
-            nc.sync.dma_start(win[:], wd_rows[:, i, :])
-            wd_win.append(win)
-
+        nc.sync.dma_start(x_raw[1][:], x_rows[:, :, HALF:T])
 
         ident_f = keep.tile([P, P], F32, name="ident_f")
         make_identity(nc, ident_f[:])
@@ -80,110 +68,119 @@ def tile_list_hot_neurons_product_pl_kernel(
         warm = keep.tile([P, 1], F32, name="warm")
         nc.scalar.activation(warm[:], ident_b[:, 0:1], ACT.Sigmoid)
 
-        rw_ps = ps_t.tile([P, PACK, P], F32, name="turned")
-        for c in range(PACK):
-            nc.tensor.transpose(rw_ps[:, c, :], rw_col[:, c : c + 1].to_broadcast([P, P]), ident_f[:])
-        rw_all = keep.tile([P, P, PACK], F32, name="rw_all")
-        nc.scalar.copy(rw_all[:], rw_ps[:].rearrange("p c n -> p n c"))
-        rw_row = rw_all[:].rearrange("p n c -> p (n c)")
-
-        su_got = keep.tile([P, J], U8, name="su_got")
-        nc.vector.tensor_copy(su_got[:], su_win[:].indirect(offsets[:]))
-        sg_got = keep.tile([P, J], U8, name="sg_got", tag="sg_got")
-        nc.vector.tensor_copy(sg_got[:], sg_win[:].indirect(offsets[:]))
-
         def deal(dst, src):
             nc.vector.tensor_copy(
                 dst.bitcast(I32).rearrange("p (t b w) -> p t b w", t=PACK, b=BLOCKS),
                 src.bitcast(I32).rearrange("p (b t w) -> p t b w", t=PACK, b=BLOCKS),
             )
 
-        s_dealt = keep.tile([P, 2 * J], U8, name="s_dealt")
-        deal(s_dealt[:, 0:J], su_got[:])
-        deal(s_dealt[:, J : 2 * J], sg_got[:])
-        for q in range(4):
+        sg_got = keep.tile([P, J], U8, name="sg_got", tag="got_first")
+        nc.vector.tensor_copy(sg_got[:], sg_win[:].indirect(offsets[:]))
+        sg_dealt = keep.tile([P, J], U8, name="sg_dealt", tag="x_bf1", align_bytes=64)
+        deal(sg_dealt[:], sg_got[:])
+        for q in (0, 2, 1, 3):
             nc.sync.dma_start(
-                w_scales[32 * q : 32 * q + 4, :].bitcast(I32), s_dealt[32 * q : 32 * q + 32 : 8, :].bitcast(I32)
+                wg_plane[32 * q : 32 * q + 4, :].bitcast(I32), sg_dealt[32 * q : 32 * q + 32 : 8, :].bitcast(I32)
             )
+        wd_rows = wd.rearrange("(p i) r -> p i r", i=PACK)
+        wd_win = [keep.tile([P, R], F32, name="wd_win%d" % i, tag="wd_win%d" % i, align_bytes=64) for i in range(PACK - 1)]
+        wd_win.append(late.tile([P, R], F32, name="wd_last", offset=0))
         for i in range(PACK):
-            load_wd(i, "wd%d" % i)
+            nc.sync.dma_start(wd_win[i][:], wd_rows[:, i, :])
+        rw_col = keep.tile([P, PACK], F32, name="rw_col")
+        nc.sync.dma_start(rw_col[:], rw[0].rearrange("(p c) -> p c", c=PACK))
 
-        wu_got = keep.tile([P, J], U16, name="wu_got", tag="sg_got")
+        wu_got = keep.tile([P, J], U16, name="wu_got", tag="sg_win")
         nc.vector.tensor_copy(wu_got[:], wu_win[:].indirect(offsets[:]))
-        wu_codes = keep.tile([P, J], U16, name="wu_codes", align_bytes=64)
+        su_got = keep.tile([P, J], U8, name="su_got", tag="got_first")
+        nc.vector.tensor_copy(su_got[:], su_win[:].indirect(offsets[:]))
+        wu_codes = keep.tile([P, J], U16, name="wu_codes", tag="su_win", align_bytes=64)
         deal(wu_codes[:], wu_got[:])
+        wu_plane = keep.tile([P, J], U8, name="wu_plane", align_bytes=64)
+        deal(wu_plane[:], su_got[:])
+
+        def weave(copy, dst, src):
+            copy(dst.rearrange("p (g n) i -> p g i n", n=GROUP), src.rearrange("p i (g n) -> p g i n", n=GROUP))
+
         x_codes, x_scales = [], []
 
-        def quantise_x(h):
-            xb = keep.tile([P, T // 2, PACK], BF16, name="x_bf%d" % h, align_bytes=64)
-            weave_x = nc.scalar.copy if h == 0 else nc.vector.tensor_copy
-            weave_x(
-                xb[:].rearrange("p (g n) i -> p g i n", n=4),
-                x_raw[h][:].rearrange("p i (g n) -> p g i n", n=4),
-            )
-            xc = keep.tile([P, T // 2], U32, name="x_codes%d" % h, align_bytes=64)
-            xs = keep.tile([P, T // 2], U8, name="x_scales%d" % h, align_bytes=64)
+        def quantise_x(h, copy):
+            xb = keep.tile([P, HALF, PACK], BF16, name="x_bf%d" % h, tag="x_bf%d" % h, align_bytes=64)
+            weave(copy, xb[:], x_raw[h][:])
+            xc = keep.tile([P, HALF], U32, name="x_codes%d" % h, align_bytes=64)
+            xs = keep.tile([P, HALF], U8, name="x_scales%d" % h, align_bytes=64)
             nc.vector.quantize_mx(xc[:].bitcast(FP8X4), xs[:], xb[:].rearrange("p n i -> p (n i)"))
             for c in range(2):
                 x_codes.append(xc[:, c * CHUNK : (c + 1) * CHUNK])
                 x_scales.append(xs[:, c * CHUNK : (c + 1) * CHUNK])
 
-        quantise_x(0)
-        wg_codes = keep.tile([P, J], U32, name="wg_codes", align_bytes=64)
+        quantise_x(0, nc.scalar.copy)
+        wg_codes = keep.tile([P, J], U32, name="wg_codes", tag="x_bf0", align_bytes=64)
         nc.vector.tensor_copy(
             wg_codes[:].rearrange("p (t b r) -> p b t r", t=PACK, r=RUN),
             wg_win[:].bitcast(U32).indirect(offsets[:]),
         )
+        quantise_x(1, nc.vector.tensor_copy)
 
-        quantise_x(1)
+        def products(bank, codes, dtype, plane, c):
+            for t in range(PACK):
+                cols = slice(t * P, (t + 1) * P)
+                nc.tensor.matmul_mx(
+                    bank[:, t, :],
+                    lhsT=codes[:, cols].bitcast(dtype),
+                    lhsT_scale=plane[:, cols],
+                    rhs=x_codes[c].bitcast(FP8X4),
+                    rhs_scale=x_scales[c],
+                    start=True,
+                    stop=True,
+                )
 
+        def first_sums(c):
+            a_ps = ps_a.tile([P, PACK, CHUNK], F32, name="a_ps")
+            b_ps = ps_b.tile([P, PACK, CHUNK], F32, name="b_ps", tag="wide")
+            products(a_ps, wu_codes, FP4X4, wu_plane, c)
+            products(b_ps, wg_codes, FP8X4, wg_plane, c)
+            return a_ps, b_ps
+
+        def gate_of(a_ps, tag):
+            gate = keep.tile([P, CHUNK, PACK], F32, name="gate", tag=tag, align_bytes=64)
+            nc.scalar.activation(gate[:], a_ps[:].rearrange("p t n -> p n t"), ACT.Sigmoid)
+            return gate
+
+        hid = []
         h_codes = keep.tile([P, T], U32, name="h_codes", align_bytes=64)
         h_scales = keep.tile([P, T], U8, name="h_scales", align_bytes=64)
 
-        def first_stage(c, gate_tag):
-            a_ps = ps_a.tile([P, PACK, CHUNK], F32, name="a_ps")
-            b_ps = ps_b.tile([P, PACK, CHUNK], F32, name="b_ps", tag="wide")
-            for t in range(PACK):
-                nc.tensor.matmul_mx(
-                    a_ps[:, t, :],
-                    lhsT=wu_codes[:, t * P : (t + 1) * P].bitcast(FP4X4),
-                    lhsT_scale=w_scales[:, t * P : (t + 1) * P],
-                    rhs=x_codes[c].bitcast(FP8X4),
-                    rhs_scale=x_scales[c],
-                    start=True,
-                    stop=True,
-                )
-            for t in range(PACK):
-                nc.tensor.matmul_mx(
-                    b_ps[:, t, :],
-                    lhsT=wg_codes[:, t * P : (t + 1) * P].bitcast(FP8X4),
-                    lhsT_scale=w_scales[:, J + t * P : J + (t + 1) * P],
-                    rhs=x_codes[c].bitcast(FP8X4),
-                    rhs_scale=x_scales[c],
-                    start=True,
-                    stop=True,
-                )
-            gate = keep.tile([P, CHUNK, PACK], F32, name="gate%d" % c, tag=gate_tag)
-            nc.scalar.activation(gate[:], a_ps[:].rearrange("p t n -> p n t"), ACT.Sigmoid)
-            return b_ps, gate
-
-        def hidden(hid, b_ps, gate):
-            nc.vector.tensor_tensor(hid, b_ps[:].rearrange("p t n -> p n t"), gate[:], MULT)
-
-        def quantise_hid(h, hid):
-            cols = slice(h * 2 * CHUNK, (h + 1) * 2 * CHUNK)
-            nc.vector.quantize_mx(
-                h_codes[:, cols].bitcast(FP8X4), h_scales[:, cols], hid[:].rearrange("p n t -> p (n t)")
+        def hidden(c, b_ps, gate):
+            lo = (c % 2) * CHUNK
+            nc.vector.tensor_tensor(
+                hid[c // 2][:, lo : lo + CHUNK, :], b_ps[:].rearrange("p t n -> p n t"), gate[:], MULT
             )
 
-        def gather_wd(i, got_tag):
-            got = keep.tile([P, 2, P, 2], BF16, name="d_got%d" % i, tag=got_tag)
+        def quantise_hid(h):
+            cols = slice(h * HALF, (h + 1) * HALF)
+            nc.vector.quantize_mx(
+                h_codes[:, cols].bitcast(FP8X4), h_scales[:, cols], hid[h][:].rearrange("p n t -> p (n t)")
+            )
+
+        def gather_and_turn_on_scalar(cast, d_bf):
+            got = keep.tile([P, PACK, P], BF16, name="d_got0")
+            nc.scalar.activation(
+                got[:].rearrange("p t (b r) -> p b t r", r=RUN), cast[:].indirect(offsets[:]), ACT.Copy
+            )
+            turned = ps_t.tile([P, PACK, P], BF16, name="turned")
+            for t in range(PACK):
+                nc.tensor.transpose(turned[:, t, :], got[:, t, :], ident_b[:])
+            nc.scalar.copy(d_bf, turned[:].rearrange("p t m -> p m t"))
+
+        def gather_pairs(i):
+            got = keep.tile([P, 2, P, 2], BF16, name="d_got%d" % i)
             nc.vector.tensor_copy(
                 got[:].rearrange("p u (b r) e -> p b u e r", r=RUN), wd_win[i][:].indirect(offsets[:])
             )
             return got
 
-        def turn(got, d_bf):
+        def turn_pairs(got, d_bf):
             words = got[:].rearrange("p u q e -> p (u q e)").bitcast(F32)
             turned = ps_t.tile([P, 2, P], F32, name="turned")
             for u in range(2):
@@ -193,32 +190,20 @@ def tile_list_hot_neurons_product_pl_kernel(
                 turned[:].rearrange("p u m -> p m u"),
             )
 
-        def gather_and_turn_on_scalar(i, d_bf):
-            cast = keep.tile([P, R], BF16, name="wd_cast")
-            nc.scalar.activation(cast[:], wd_win[i][:], ACT.Copy)
-            got = keep.tile([P, PACK, P], BF16, name="d_got_scalar")
-            nc.scalar.activation(
-                got[:].rearrange("p t (b r) -> p b t r", r=RUN), cast[:].indirect(offsets[:]), ACT.Copy
-            )
-            turned = ps_t.tile([P, PACK, P], BF16, name="turned")
-            for t in range(PACK):
-                nc.tensor.transpose(turned[:, t, :], got[:, t, :], ident_b[:])
-            nc.scalar.copy(d_bf, turned[:].rearrange("p t m -> p m t"))
-
-        def quantise_d(dc, ds, d_bf):
-            nc.vector.quantize_mx(dc.bitcast(FP8X4), ds, d_bf.rearrange("p m t -> p (m t)"))
+        def quantise_d(codes, plane, d_bf):
+            nc.vector.quantize_mx(codes.bitcast(FP8X4), plane, d_bf.rearrange("p m t -> p (m t)"))
 
         out_rows = out_0.rearrange("(p i) t -> p i t", i=PACK)
 
-        def second_stage(i, dc, ds, parts):
+        def second_stage(i, codes, plane, parts):
             width = T // parts
             for h in range(parts):
                 cols = slice(h * width, (h + 1) * width)
                 p_ps = ps_b.tile([P, width], F32, name="p_ps", tag="wide")
                 nc.tensor.matmul_mx(
                     p_ps[:],
-                    lhsT=dc.bitcast(FP8X4),
-                    lhsT_scale=ds,
+                    lhsT=codes.bitcast(FP8X4),
+                    lhsT_scale=plane,
                     rhs=h_codes[:, cols].bitcast(FP8X4),
                     rhs_scale=h_scales[:, cols],
                     start=True,
@@ -227,63 +212,66 @@ def tile_list_hot_neurons_product_pl_kernel(
                 nc.vector.tensor_tensor(y[:, i, cols], p_ps[:], rw_row[:, cols], MULT)
             nc.sync.dma_start(out_rows[:, i, :], y[:, i, :])
 
-        d_bf0 = keep.tile([P, P, PACK], BF16, name="d_bf0", align_bytes=64)
-        d_bf12 = keep.tile([P, 2 * P, PACK], BF16, name="d_bf12", align_bytes=64)
+        d_bf02 = keep.tile([P, 2 * P, PACK], BF16, name="d_bf02", align_bytes=64)
+        d_bf1 = keep.tile([P, P, PACK], BF16, name="d_bf1", align_bytes=64)
         d_bf3 = keep.tile([P, P, PACK], BF16, name="d_bf3", align_bytes=64)
-        dc0 = keep.tile([P, P], U32, name="dc0", align_bytes=64)
-        ds0 = keep.tile([P, P], U8, name="ds0", align_bytes=64)
-        dc3 = keep.tile([P, P], U32, name="dc3", align_bytes=64)
+        ds02 = keep.tile([P, 2 * P], U8, name="ds02", align_bytes=64)
+        ds1 = keep.tile([P, P], U8, name="ds1", align_bytes=64)
         ds3 = keep.tile([P, P], U8, name="ds3", align_bytes=64)
-        ds12 = keep.tile([P, 2 * P], U8, name="ds12", align_bytes=64)
+        dc3 = keep.tile([P, P], U32, name="dc3", align_bytes=64)
+        for h in range(2):
+            hid.append(keep.tile([P, HALF, PACK], BF16, name="hid%d" % h, align_bytes=64))
 
-        sums = [first_stage(c, "gate%d" % c) for c in range(N_CHUNKS)]
-        hid_a = keep.tile([P, 2 * CHUNK, PACK], BF16, name="hid_a", align_bytes=64)
-        hid_b = keep.tile([P, 2 * CHUNK, PACK], BF16, name="hid_b", align_bytes=64)
-        y = keep.tile([P, PACK, T], F32, name="y")
-        hidden(hid_a[:, 0:CHUNK, :], *sums[0])
-        got0 = gather_wd(0, "gate0")
-        hidden(hid_a[:, CHUNK : 2 * CHUNK, :], *sums[1])
-        hidden(hid_b[:, 0:CHUNK, :], *sums[2])
-        quantise_hid(0, hid_a)
-        hidden(hid_b[:, CHUNK : 2 * CHUNK, :], *sums[3])
-        turn(got0, d_bf0[:])
-        quantise_d(dc0[:], ds0[:], d_bf0[:])
-        quantise_hid(1, hid_b)
-        gather_and_turn_on_scalar(1, d_bf12[:, 0:P, :])
-        turn(gather_wd(2, "got2"), d_bf12[:, P : 2 * P, :])
-        second_stage(0, dc0[:], ds0[:], 1)
-        turn(gather_wd(3, "got3"), d_bf3[:])
-        dc12 = late.tile([P, 2 * P], U32, name="dc12", offset=0, align_bytes=64)
-        quantise_d(dc12[:], ds12[:], d_bf12[:])
-        second_stage(1, dc12[:, 0:P], ds12[:, 0:P], 1)
+        for c in range(2):
+            a_ps, b_ps = first_sums(c)
+            hidden(c, b_ps, gate_of(a_ps, "gate%d" % c))
+        quantise_hid(0)
+        cast = keep.tile([P, R], BF16, name="wd_cast")
+        nc.scalar.activation(cast[:], wd_win[0][:], ACT.Copy)
+        sums = [first_sums(c) for c in (2, 3)]
+        gates = [gate_of(sums[0][0], "wd_win0"), gate_of(sums[1][0], "gate3")]
+        got1 = gather_pairs(1)
+        hidden(2, sums[0][1], gates[0])
+        hidden(3, sums[1][1], gates[1])
+        turn_pairs(got1, d_bf1[:])
+        gather_and_turn_on_scalar(cast, d_bf02[:, 0:P, :])
+        quantise_hid(1)
+        got2 = gather_pairs(2)
+        dc1 = keep.tile([P, P], U32, name="dc1", tag="wd_win2", align_bytes=64)
+        quantise_d(dc1[:], ds1[:], d_bf1[:])
+        turn_pairs(got2, d_bf02[:, P : 2 * P, :])
+        rw_ps = ps_t.tile([P, PACK, P], F32, name="turned")
+        for c in range(PACK):
+            nc.tensor.transpose(rw_ps[:, c, :], rw_col[:, c : c + 1].to_broadcast([P, P]), ident_f[:])
+        rw_all = keep.tile([P, P, PACK], F32, name="rw_all")
+        nc.scalar.copy(rw_all[:], rw_ps[:].rearrange("p c n -> p n c"))
+        rw_row = rw_all[:].rearrange("p n c -> p (n c)")
+        turn_pairs(gather_pairs(3), d_bf3[:])
+        dc02 = late.tile([P, 2 * P], U32, name="dc02", offset=0, align_bytes=64)
+        y = late.tile([P, PACK, T], F32, name="y", offset=1024)
+        quantise_d(dc02[:], ds02[:], d_bf02[:])
+        second_stage(1, dc1[:], ds1[:], 1)
         quantise_d(dc3[:], ds3[:], d_bf3[:])
-        second_stage(2, dc12[:, P : 2 * P], ds12[:, P : 2 * P], 1)
+        second_stage(0, dc02[:, 0:P], ds02[:, 0:P], 1)
+        y_bf = [keep.tile([P, HALF, PACK], BF16, name="y_bf%d" % h, align_bytes=64) for h in range(2)]
+        for h in range(2):
+            weave(nc.scalar.copy, y_bf[h][:, :, 0:2], y[:, 0:2, h * HALF : (h + 1) * HALF])
+        second_stage(2, dc02[:, P : 2 * P], ds02[:, P : 2 * P], 1)
         second_stage(3, dc3[:], ds3[:], 2)
 
         y_codes = keep.tile([P, T], U32, name="y_codes", align_bytes=64)
         y_scales = keep.tile([P, T], U8, name="y_scales", align_bytes=64)
-        half = T // 2
         words_out = out_1[0].rearrange("p n t -> p (n t)").bitcast(I32)
-        y_bf = [keep.tile([P, half, PACK], BF16, name="y_bf%d" % h, align_bytes=64) for h in range(2)]
-
-        def weave(copy, h, lo, hi):
-            copy(
-                y_bf[h][:, lo:hi, :].rearrange("p (g n) i -> p g i n", n=4),
-                y[:, :, h * half + lo : h * half + hi].rearrange("p i (g n) -> p g i n", n=4),
-            )
-
-        split = 160
-        weave(nc.scalar.copy, 0, 0, split)
-        weave(nc.vector.tensor_copy, 1, 0, half)
-        weave(nc.vector.tensor_copy, 0, split, half)
-        for h in (1, 0):
-            cols = slice(h * half, (h + 1) * half)
+        for h in range(2):
+            weave(nc.vector.tensor_copy, y_bf[h][:, :, 2:4], y[:, 2:4, h * HALF : (h + 1) * HALF])
+        for h in range(2):
+            cols = slice(h * HALF, (h + 1) * HALF)
             nc.vector.quantize_mx(
                 y_codes[:, cols].bitcast(FP8X4), y_scales[:, cols], y_bf[h][:].rearrange("p n i -> p (n i)")
             )
             nc.sync.dma_start(words_out[:, cols], y_codes[:, cols].bitcast(I32))
         for q in range(4):
-            eng = nc.scalar if q % 2 == 0 else nc.sync
-            eng.dma_start(
+            queue = nc.scalar if q % 2 == 0 else nc.sync
+            queue.dma_start(
                 out_2[0, 4 * q : 4 * q + 4, :].bitcast(I32), y_scales[32 * q : 32 * q + 4, :].bitcast(I32)
             )

from contextlib import ExitStack

import concourse.mybir as mybir
from concourse.masks import make_identity

K, T, R, J, M = 512, 512, 2048, 512, 512
FLOPS = 2 * (2 * K * J * T + J * M * T)

F32 = mybir.dt.float32
BF16 = mybir.dt.bfloat16
I32 = mybir.dt.int32
U32 = mybir.dt.uint32
U16 = mybir.dt.uint16
U8 = mybir.dt.uint8
FP8X4 = mybir.dt.float8_e4m3fn_x4
FP4X4 = mybir.dt.float4_e2m1fn_x4
ACT = mybir.ActivationFunctionType
MULT = mybir.AluOpType.mult

P = 128
PACK = 4
CHUNK = 128
HALF = T // 2
BLOCKS = J // 32
RUN = 8
GROUP = 4


def tile_list_hot_neurons_product_pl_kernel(
    tc, xt, wu_words, wu_scales, wg_words, wg_scales, wd, rw, offs, out_0, out_1, out_2
):
    nc = tc.nc
    with ExitStack() as ctx:
        keep = ctx.enter_context(tc.tile_pool(name="keep", bufs=1))
        late = ctx.enter_context(tc.tile_pool(name="late", bufs=1))
        ps_a = ctx.enter_context(tc.psum_pool(name="ps_a", bufs=2))
        ps_b = ctx.enter_context(tc.psum_pool(name="ps_b", bufs=4))
        ps_t = ctx.enter_context(tc.psum_pool(name="ps_t", bufs=2))

        offsets = keep.tile([P, J // 16], U16, name="offsets")
        nc.sync.dma_start(offsets[:], offs)

        su_win = keep.tile([P, R], U8, name="su_win", tag="su_win", align_bytes=64)
        sg_win = keep.tile([P, R], U8, name="sg_win", tag="sg_win")
        wg_plane = keep.tile([P, J], U8, name="wg_plane", align_bytes=64)
        nc.gpsimd.memset(sg_win[:].bitcast(I32), 0)
        nc.vector.memset(su_win[:].bitcast(I32), 0)
        nc.vector.memset(wg_plane[:].bitcast(I32), 0)

        wu_win = keep.tile([P, R], U16, name="wu_win")
        nc.sync.dma_start(wu_win[:].bitcast(I32), wu_words[0].bitcast(I32))
        nc.sync.dma_start(sg_win[0:P:8, :].bitcast(I32), wg_scales[0].bitcast(I32))
        for q in (0, 2, 1, 3):
            nc.sync.dma_start(
                su_win[32 * q : 32 * q + 4, :].bitcast(I32), wu_scales[0, 4 * q : 4 * q + 4, :].bitcast(I32)
            )
        x_rows = xt.rearrange("(p i) t -> p i t", i=PACK)
        x_raw = [keep.tile([P, PACK, HALF], F32, name="x_raw%d" % h) for h in range(2)]
        nc.sync.dma_start(x_raw[0][:], x_rows[:, :, 0:HALF])
        wg_win = keep.tile([P, R], I32, name="wg_win")
        nc.sync.dma_start(wg_win[:], wg_words[0].rearrange("p n t -> p (n t)").bitcast(I32))
        nc.sync.dma_start(x_raw[1][:], x_rows[:, :, HALF:T])

        ident_f = keep.tile([P, P], F32, name="ident_f")
        make_identity(nc, ident_f[:])
        ident_b = keep.tile([P, P], BF16, name="ident_b")
        make_identity(nc, ident_b[:])
        warm = keep.tile([P, 1], F32, name="warm")
        nc.scalar.activation(warm[:], ident_b[:, 0:1], ACT.Sigmoid)

        def deal(dst, src):
            nc.vector.tensor_copy(
                dst.bitcast(I32).rearrange("p (t b w) -> p t b w", t=PACK, b=BLOCKS),
                src.bitcast(I32).rearrange("p (b t w) -> p t b w", t=PACK, b=BLOCKS),
            )

        sg_got = keep.tile([P, J], U8, name="sg_got", tag="got_first")
        nc.vector.tensor_copy(sg_got[:], sg_win[:].indirect(offsets[:]))
        sg_dealt = keep.tile([P, J], U8, name="sg_dealt", tag="x_bf1", align_bytes=64)
        deal(sg_dealt[:], sg_got[:])
        for q in (0, 2, 1, 3):
            nc.sync.dma_start(
                wg_plane[32 * q : 32 * q + 4, :].bitcast(I32), sg_dealt[32 * q : 32 * q + 32 : 8, :].bitcast(I32)
            )
        wd_rows = wd.rearrange("(p i) r -> p i r", i=PACK)
        wd_win = [keep.tile([P, R], F32, name="wd_win%d" % i, tag="wd_win%d" % i, align_bytes=64) for i in range(PACK - 1)]
        wd_win.append(late.tile([P, R], F32, name="wd_last", offset=0))
        for i in range(PACK):
            nc.sync.dma_start(wd_win[i][:], wd_rows[:, i, :])
        rw_col = keep.tile([P, PACK], F32, name="rw_col")
        nc.sync.dma_start(rw_col[:], rw[0].rearrange("(p c) -> p c", c=PACK))

        wu_got = keep.tile([P, J], U16, name="wu_got", tag="sg_win")
        nc.vector.tensor_copy(wu_got[:], wu_win[:].indirect(offsets[:]))
        su_got = keep.tile([P, J], U8, name="su_got", tag="got_first")
        nc.vector.tensor_copy(su_got[:], su_win[:].indirect(offsets[:]))
        wu_codes = keep.tile([P, J], U16, name="wu_codes", tag="su_win", align_bytes=64)
        deal(wu_codes[:], wu_got[:])
        wu_plane = keep.tile([P, J], U8, name="wu_plane", align_bytes=64)
        deal(wu_plane[:], su_got[:])

        def weave(copy, dst, src):
            copy(dst.rearrange("p (g n) i -> p g i n", n=GROUP), src.rearrange("p i (g n) -> p g i n", n=GROUP))

        x_codes, x_scales = [], []

        def quantise_x(h, copy):
            xb = keep.tile([P, HALF, PACK], BF16, name="x_bf%d" % h, tag="x_bf%d" % h, align_bytes=64)
            weave(copy, xb[:], x_raw[h][:])
            xc = keep.tile([P, HALF], U32, name="x_codes%d" % h, align_bytes=64)
            xs = keep.tile([P, HALF], U8, name="x_scales%d" % h, align_bytes=64)
            nc.vector.quantize_mx(xc[:].bitcast(FP8X4), xs[:], xb[:].rearrange("p n i -> p (n i)"))
            for c in range(2):
                x_codes.append(xc[:, c * CHUNK : (c + 1) * CHUNK])
                x_scales.append(xs[:, c * CHUNK : (c + 1) * CHUNK])

        quantise_x(0, nc.scalar.copy)
        wg_codes = keep.tile([P, J], U32, name="wg_codes", tag="x_bf0", align_bytes=64)
        nc.vector.tensor_copy(
            wg_codes[:].rearrange("p (t b r) -> p b t r", t=PACK, r=RUN),
            wg_win[:].bitcast(U32).indirect(offsets[:]),
        )
        quantise_x(1, nc.vector.tensor_copy)

        def products(bank, codes, dtype, plane, c):
            for t in range(PACK):
                cols = slice(t * P, (t + 1) * P)
                nc.tensor.matmul_mx(
                    bank[:, t, :],
                    lhsT=codes[:, cols].bitcast(dtype),
                    lhsT_scale=plane[:, cols],
                    rhs=x_codes[c].bitcast(FP8X4),
                    rhs_scale=x_scales[c],
                    start=True,
                    stop=True,
                )

        def first_sums(c):
            a_ps = ps_a.tile([P, PACK, CHUNK], F32, name="a_ps")
            b_ps = ps_b.tile([P, PACK, CHUNK], F32, name="b_ps", tag="wide")
            products(a_ps, wu_codes, FP4X4, wu_plane, c)
            products(b_ps, wg_codes, FP8X4, wg_plane, c)
            return a_ps, b_ps

        def gate_of(a_ps, tag):
            gate = keep.tile([P, CHUNK, PACK], F32, name="gate", tag=tag, align_bytes=64)
            nc.scalar.activation(gate[:], a_ps[:].rearrange("p t n -> p n t"), ACT.Sigmoid)
            return gate

        hid = []
        h_codes = keep.tile([P, T], U32, name="h_codes", align_bytes=64)
        h_scales = keep.tile([P, T], U8, name="h_scales", align_bytes=64)

        def hidden(c, b_ps, gate):
            lo = (c % 2) * CHUNK
            nc.vector.tensor_tensor(
                hid[c // 2][:, lo : lo + CHUNK, :], b_ps[:].rearrange("p t n -> p n t"), gate[:], MULT
            )

        def quantise_hid(h):
            cols = slice(h * HALF, (h + 1) * HALF)
            nc.vector.quantize_mx(
                h_codes[:, cols].bitcast(FP8X4), h_scales[:, cols], hid[h][:].rearrange("p n t -> p (n t)")
            )

        def gather_and_turn_on_scalar(cast, d_bf):
            got = keep.tile([P, PACK, P], BF16, name="d_got0")
            nc.scalar.activation(
                got[:].rearrange("p t (b r) -> p b t r", r=RUN), cast[:].indirect(offsets[:]), ACT.Copy
            )
            turned = ps_t.tile([P, PACK, P], BF16, name="turned")
            for t in range(PACK):
                nc.tensor.transpose(turned[:, t, :], got[:, t, :], ident_b[:])
            nc.scalar.copy(d_bf, turned[:].rearrange("p t m -> p m t"))

        def gather_pairs(i):
            got = keep.tile([P, 2, P, 2], BF16, name="d_got%d" % i)
            nc.vector.tensor_copy(
                got[:].rearrange("p u (b r) e -> p b u e r", r=RUN), wd_win[i][:].indirect(offsets[:])
            )
            return got

        def turn_pairs(got, d_bf):
            words = got[:].rearrange("p u q e -> p (u q e)").bitcast(F32)
            turned = ps_t.tile([P, 2, P], F32, name="turned")
            for u in range(2):
                nc.tensor.transpose(turned[:, u, :], words[:, u * P : (u + 1) * P], ident_f[:])
            nc.scalar.copy(
                d_bf.rearrange("p m t -> p (m t)").bitcast(F32).rearrange("p (m u) -> p m u", u=2),
                turned[:].rearrange("p u m -> p m u"),
            )

        def quantise_d(codes, plane, d_bf):
            nc.vector.quantize_mx(codes.bitcast(FP8X4), plane, d_bf.rearrange("p m t -> p (m t)"))

        out_rows = out_0.rearrange("(p i) t -> p i t", i=PACK)

        def second_stage(i, codes, plane, parts):
            width = T // parts
            for h in range(parts):
                cols = slice(h * width, (h + 1) * width)
                p_ps = ps_b.tile([P, width], F32, name="p_ps", tag="wide")
                nc.tensor.matmul_mx(
                    p_ps[:],
                    lhsT=codes.bitcast(FP8X4),
                    lhsT_scale=plane,
                    rhs=h_codes[:, cols].bitcast(FP8X4),
                    rhs_scale=h_scales[:, cols],
                    start=True,
                    stop=True,
                )
                nc.vector.tensor_tensor(y[:, i, cols], p_ps[:], rw_row[:, cols], MULT)
            nc.sync.dma_start(out_rows[:, i, :], y[:, i, :])

        d_bf02 = keep.tile([P, 2 * P, PACK], BF16, name="d_bf02", align_bytes=64)
        d_bf1 = keep.tile([P, P, PACK], BF16, name="d_bf1", align_bytes=64)
        d_bf3 = keep.tile([P, P, PACK], BF16, name="d_bf3", align_bytes=64)
        ds02 = keep.tile([P, 2 * P], U8, name="ds02", align_bytes=64)
        ds1 = keep.tile([P, P], U8, name="ds1", align_bytes=64)
        ds3 = keep.tile([P, P], U8, name="ds3", align_bytes=64)
        dc3 = keep.tile([P, P], U32, name="dc3", align_bytes=64)
        for h in range(2):
            hid.append(keep.tile([P, HALF, PACK], BF16, name="hid%d" % h, align_bytes=64))

        for c in range(2):
            a_ps, b_ps = first_sums(c)
            hidden(c, b_ps, gate_of(a_ps, "gate%d" % c))
        quantise_hid(0)
        cast = keep.tile([P, R], BF16, name="wd_cast")
        nc.scalar.activation(cast[:], wd_win[0][:], ACT.Copy)
        sums = [first_sums(c) for c in (2, 3)]
        gates = [gate_of(sums[0][0], "wd_win0"), gate_of(sums[1][0], "gate3")]
        got1 = gather_pairs(1)
        hidden(2, sums[0][1], gates[0])
        hidden(3, sums[1][1], gates[1])
        turn_pairs(got1, d_bf1[:])
        gather_and_turn_on_scalar(cast, d_bf02[:, 0:P, :])
        quantise_hid(1)
        got2 = gather_pairs(2)
        dc1 = keep.tile([P, P], U32, name="dc1", tag="wd_win2", align_bytes=64)
        quantise_d(dc1[:], ds1[:], d_bf1[:])
        turn_pairs(got2, d_bf02[:, P : 2 * P, :])
        rw_ps = ps_t.tile([P, PACK, P], F32, name="turned")
        for c in range(PACK):
            nc.tensor.transpose(rw_ps[:, c, :], rw_col[:, c : c + 1].to_broadcast([P, P]), ident_f[:])
        rw_all = keep.tile([P, P, PACK], F32, name="rw_all")
        nc.scalar.copy(rw_all[:], rw_ps[:].rearrange("p c n -> p n c"))
        rw_row = rw_all[:].rearrange("p n c -> p (n c)")
        turn_pairs(gather_pairs(3), d_bf3[:])
        dc02 = late.tile([P, 2 * P], U32, name="dc02", offset=0, align_bytes=64)
        y = late.tile([P, PACK, T], F32, name="y", offset=1024)
        quantise_d(dc02[:], ds02[:], d_bf02[:])
        second_stage(1, dc1[:], ds1[:], 1)
        quantise_d(dc3[:], ds3[:], d_bf3[:])
        second_stage(0, dc02[:, 0:P], ds02[:, 0:P], 1)
        y_bf = [keep.tile([P, HALF, PACK], BF16, name="y_bf%d" % h, align_bytes=64) for h in range(2)]
        for h in range(2):
            weave(nc.scalar.copy, y_bf[h][:, :, 0:2], y[:, 0:2, h * HALF : (h + 1) * HALF])
        second_stage(2, dc02[:, P : 2 * P], ds02[:, P : 2 * P], 1)
        second_stage(3, dc3[:], ds3[:], 2)

        y_codes = keep.tile([P, T], U32, name="y_codes", align_bytes=64)
        y_scales = keep.tile([P, T], U8, name="y_scales", align_bytes=64)
        words_out = out_1[0].rearrange("p n t -> p (n t)").bitcast(I32)
        for h in range(2):
            weave(nc.vector.tensor_copy, y_bf[h][:, :, 2:4], y[:, 2:4, h * HALF : (h + 1) * HALF])
        for h in range(2):
            cols = slice(h * HALF, (h + 1) * HALF)
            nc.vector.quantize_mx(
                y_codes[:, cols].bitcast(FP8X4), y_scales[:, cols], y_bf[h][:].rearrange("p n i -> p (n i)")
            )
            nc.sync.dma_start(words_out[:, cols], y_codes[:, cols].bitcast(I32))
        for q in range(4):
            queue = nc.scalar if q % 2 == 0 else nc.sync
            queue.dma_start(
                out_2[0, 4 * q : 4 * q + 4, :].bitcast(I32), y_scales[32 * q : 32 * q + 4, :].bitcast(I32)
            )
